import numpy as np
import ml_dtypes


def mxq(x, axis, fmt="e4m3"):
    dtype, down = {"e4m3": (ml_dtypes.float8_e4m3fn, 7), "e5m2": (ml_dtypes.float8_e5m2, 14)}[fmt]
    v = np.moveaxis(np.asarray(x, np.float32).astype(ml_dtypes.bfloat16).astype(np.float64), axis, -1)
    blocks = v.reshape(v.shape[:-1] + (-1, 32))
    amax = np.abs(blocks).max(-1, keepdims=True)
    byte = np.maximum(np.where(amax > 0, np.frexp(amax)[1] - 1 + 127, 0) - down, 1)
    scale = np.exp2(byte - 127.0)
    codes = (blocks / scale).astype(np.float32).astype(dtype).astype(np.float64)
    return np.moveaxis((codes * scale).reshape(v.shape), -1, axis)


WIDE = False


def mx_kscale(k):
    if not WIDE:
        return np.ones(k)
    levels = np.array([10, -10, 5, -5, 0])
    if k % 512:
        return np.exp2(np.random.permutation(np.resize(levels, k // 32))).repeat(32)
    a = np.empty((k // 512, 16))
    for p in range(k // 512):
        a[p, :8] = np.random.permutation(np.resize(levels, 8))
        for g in range(8):
            far = levels[np.abs(levels - a[p, g]) >= 10]
            a[p, g + 8] = far[np.random.randint(len(far))]
    return np.exp2(a.ravel()).repeat(32)


BF16 = ml_dtypes.bfloat16


def bf(x):
    return np.asarray(x, np.float32).astype(BF16)


def f64(x):
    return np.asarray(x).astype(np.float64)


N, D = 8192, 512


def draw0():
    s, t = mx_kscale(D), mx_kscale(N)
    x = np.random.standard_normal((N, D)) * s
    w = np.random.standard_normal((D, D)) / np.sqrt(D) / s[None, :]
    k = np.random.uniform(-1.0, 1.0, D)
    g = (1.0 + 0.1 * np.random.standard_normal(N)) * t
    h = (1.0 + 0.1 * np.random.standard_normal(N)) / t
    return {"x": bf(x), "w": bf(w), "k": bf(k), "g": bf(g), "h": bf(h)}


def core(x, w, k, g, h):
    n = x.shape[0]
    root_n = np.sqrt(n)
    y = mxq(f64(x), 1, "e4m3") @ mxq(f64(w), 1, "e4m3").T
    p = f64(g)[:, None] * (f64(k)[None, :] * np.tanh(y) + y)
    z = f64(h)[:, None] * y
    c = (mxq(p, 0, "e4m3").T @ mxq(z, 0, "e4m3")) / root_n
    return root_n * np.eye(w.shape[0]) - c


def e4m3fn_bytes(y):
    return np.clip(np.asarray(y, np.float64), -448.0, 448.0).astype(np.float32).astype(ml_dtypes.float8_e4m3fn).view(np.uint8)


def e4m3fn_values(b):
    return np.asarray(b, np.uint8).view(ml_dtypes.float8_e4m3fn).astype(np.float64)


def setup_inputs():
    d = draw0()
    x0 = np.asarray(d['x']).astype(np.float64)
    s = (np.max(np.abs(x0), axis=(0,), keepdims=True) / 448.0).astype(np.float32)
    out = {}
    for k, v in d.items():
        if k == 'x':
            out['x_bytes'] = e4m3fn_bytes(x0 / s.astype(np.float64))
            out['x_scale'] = s
        else:
            out[k] = v
    return out


def reference(x_bytes, x_scale, w, k, g, h):
    return core(e4m3fn_values(x_bytes) * x_scale.astype(np.float64), w, k, g, h)

@@ -1,0 +1,417 @@
+import math
+from contextlib import ExitStack
+
+import concourse.mybir as mybir
+from concourse.masks import make_identity
+
+N, D = 8192, 512
+FLOPS = 2 * (2 * N * D * D)
+
+F32 = mybir.dt.float32
+BF16 = mybir.dt.bfloat16
+U32 = mybir.dt.uint32
+U8 = mybir.dt.uint8
+E4M3FN = mybir.dt.float8_e4m3fn
+FP8X4 = mybir.dt.float8_e4m3fn_x4
+ACT = mybir.ActivationFunctionType
+ALU = mybir.AluOpType
+
+P = 128
+PACK = 4
+GROUP = P * PACK
+GROUPS = N // GROUP
+M_TILES = D // P
+ROOT_N = math.sqrt(N)
+BLOCK_T = (0, 2, 1, 3)
+YB, TB = 2, 3
+DEFER = 1
+TEMPLATE = [
+    ("tanh", 0, 1),
+    ("mix_z", -1, 0),
+    ("zt", 0, 1),
+    ("b", 0, 1),
+    ("mm_yt", 0, 2),
+    ("p", -1, 3),
+    ("cast", 3, 0),
+    ("scale_x", 2, 0),
+    ("quant_z", -1, 0),
+    ("turn_p", -1, 1),
+    ("out_p", -1, 0),
+    ("p", 0, 0),
+    ("tanh", 0, 2),
+    ("turn_z", 0, 0),
+    ("b", 0, 2),
+    ("p", 0, 1),
+    ("quantize_x", 1, 0),
+    ("mm_yt", 0, 3),
+    ("mm_c", -2, 3),
+    ("turn_x", 2, 1),
+    ("out_p", -1, 1),
+    ("mm_ys", 0, 0),
+    ("out_z", 0, 0),
+    ("tanh", 0, 3),
+    ("mm_c", -2, 2),
+    ("quant_p", -1, 0),
+    ("b", 0, 3),
+    ("cast", 3, 1),
+    ("zs", 0, 0),
+    ("scale_x", 2, 1),
+    ("mm_ys", 0, 1),
+    ("p", 0, 2),
+    ("mm_yt", 1, 0),
+    ("mm_yt", 1, 1),
+    ("mm_c", -1, 0),
+    ("tanh", 1, 0),
+    ("b", 1, 0),
+    ("turn_p", 0, 0),
+    ("mm_c", -1, 1),
+    ("zs", 0, 1),
+    ("zt", 1, 0),
+    ("turn_x", 3, 0),
+]
+
+
+def tile_extendedinfomaxnaturalgradient_t_kernel(tc, x_bytes, x_scale, w, k, g, h, out):
+    nc = tc.nc
+    with ExitStack() as ctx:
+        keep = ctx.enter_context(tc.tile_pool(name="keep", bufs=1))
+        work = ctx.enter_context(tc.tile_pool(name="work", bufs=2))
+        deep = ctx.enter_context(tc.tile_pool(name="deep", bufs=3))
+        stay = ctx.enter_context(tc.tile_pool(name="stay", bufs=GROUPS if DEFER else 4))
+        acc_pool = ctx.enter_context(tc.psum_pool(name="acc", bufs=1))
+        y_pool = ctx.enter_context(tc.psum_pool(name="yp", bufs=YB))
+        t_pool = ctx.enter_context(tc.psum_pool(name="tp", bufs=TB))
+        ctx.enter_context(tc.manual_schedule())
+
+        x_view = x_bytes.rearrange("(g p t) k -> p g (t k)", p=P, t=PACK)
+        chunks = [(0, 1), (1, 2), (2, 4), (4, 8), (8, 12), (12, 16)]
+        xb = {}
+
+        def load_x(c):
+            lo, hi = chunks[c]
+            xbytes = keep.tile([P, hi - lo, PACK * D], U8, name="xbytes%d" % c, align_bytes=64)
+            nc.sync.dma_start(out=xbytes[:], in_=x_view[:, lo:hi, :])
+            for q in range(lo, hi):
+                xb[q] = xbytes[:, q - lo, :]
+
+        gb = {}
+        hb = {}
+
+        def load_gains(c):
+            lo, hi = chunks[c]
+            g_b = keep.tile([P, hi - lo, GROUP], BF16, name="gb%d" % c)
+            h_b = keep.tile([P, hi - lo, GROUP], BF16, name="hb%d" % c)
+            rows = slice(lo * GROUP, hi * GROUP)
+            nc.sync.dma_start(out=g_b[:].rearrange("p a n -> p (a n)"), in_=g[rows].partition_broadcast(P))
+            nc.sync.dma_start(out=h_b[:].rearrange("p a n -> p (a n)"), in_=h[rows].partition_broadcast(P))
+            for q in range(lo, hi):
+                gb[q] = g_b[:, q - lo, :].rearrange("i (w u e) -> i u w e", u=2, e=2)
+                hb[q] = h_b[:, q - lo, :].rearrange("i (w u e) -> i u w e", u=2, e=2)
+
+        k_rows = keep.tile([P, P], BF16)
+        nc.vector.memset(k_rows[:], 0.0)
+        load_x(0)
+        w_rows = keep.tile([P, M_TILES, D], BF16, align_bytes=64)
+        nc.sync.dma_start(out=w_rows[:], in_=w.rearrange("(m p) j -> p m j", p=P))
+        s4 = keep.tile([P, 2, 2], F32)
+        nc.sync.dma_start(out=s4[:], in_=x_scale.rearrange("o (p u e) -> p (o u) e", u=2, e=2))
+        nc.sync.dma_start(out=k_rows[0:M_TILES, :], in_=k.rearrange("(m p) -> m p", p=P))
+        load_x(1)
+        load_gains(0)
+        load_gains(1)
+        h16 = keep.tile([P, GROUPS, PACK], BF16)
+        nc.scalar.dma_start(out=h16[:], in_=h.rearrange("(g p t) -> p g t", p=P, t=PACK))
+        for c in range(2, len(chunks)):
+            load_x(c)
+            load_gains(c)
+
+        ident = keep.tile([P, P], F32)
+        make_identity(nc, ident[:])
+        warm = keep.tile([P, 1], F32)
+        nc.vector.memset(warm[:], 0.0)
+        warm_out = keep.tile([P, 1], F32)
+        nc.scalar.activation(out=warm_out[:], in_=warm[:], func=ACT.Tanh)
+        h32 = keep.tile([P, GROUPS, PACK], F32)
+        k32 = keep.tile([P, M_TILES], F32)
+
+        wide = {}
+        grouped = {}
+        x_codes = {}
+        x_scales = {}
+        turned = {}
+        yts = {}
+        ysr = {}
+        tanhs = {}
+        bs = {}
+        pts = {}
+        zts = {}
+        p_in = {}
+        z_in = {}
+        z_rows = {}
+        p_q = {}
+        z_q = {}
+
+        def cast(q, c, pieces):
+            if c == 0:
+                x_wide = deep.tile([P, PACK * D], BF16, name="x_wide", align_bytes=64)
+                wide[q] = x_wide
+            step = PACK * D // pieces
+            cols = slice(c * step, (c + 1) * step)
+            nc.scalar.copy(out=wide[q][:, cols], in_=xb[q][:, cols].bitcast(E4M3FN))
+
+        def turn_x(q, half):
+            bank = t_pool.tile([P, 2, 2, P], F32, name="mix")
+            words = wide[q][:].bitcast(F32)
+            for a in range(2):
+                lo = BLOCK_T[2 * half + a] * (D // 2)
+                for u in range(2):
+                    nc.tensor.transpose(bank[:, u, a, :], words[:, lo + u : lo + D // 2 : 2], ident[:])
+            turned[q, half] = bank
+
+        def scale_x(q, half):
+            if half == 0:
+                x_grouped = work.tile([P, GROUP, 2, 2], BF16, name="x_grouped", align_bytes=64)
+                grouped[q] = x_grouped
+            rows = slice(half * 2 * P, (half + 1) * 2 * P)
+            bank = turned[q, half][:].rearrange("p u a r -> p (u a r)").bitcast(BF16)
+            nc.vector.tensor_tensor(
+                out=grouped[q][:, rows, :, :],
+                in0=bank.rearrange("p (u r e) -> p r u e", u=2, e=2),
+                in1=s4[:].unsqueeze(1).to_broadcast([P, 2 * P, 2, 2]),
+                op=ALU.mult,
+            )
+
+        def quantize_x(q):
+            codes = deep.tile([P, GROUP], U32, name="x_codes", align_bytes=64)
+            scales = deep.tile([P, GROUP], U8, name="x_scales", align_bytes=64)
+            nc.vector.quantize_mx(
+                out=codes[:].bitcast(FP8X4),
+                scales=scales[:],
+                in_=grouped[q][:].rearrange("p r u e -> p (r u e)"),
+            )
+            x_codes[q] = codes
+            x_scales[q] = scales
+
+        def mm_yt(q, m):
+            yt = y_pool.tile([P, GROUP], F32, name="yt")
+            cols = slice(m * P, (m + 1) * P)
+            nc.tensor.matmul_mx(
+                out=yt[:],
+                lhsT=w_codes[:, cols].bitcast(FP8X4),
+                lhsT_scale=w_scales[:, cols],
+                rhs=x_codes[q][:].bitcast(FP8X4),
+                rhs_scale=x_scales[q][:],
+                start=True,
+                stop=True,
+            )
+            yts[q, m] = yt
+
+        def mm_ys(q, half):
+            bank = t_pool.tile([P, 2, 2 * P], F32, name="mix")
+            for a in range(2):
+                cols = slice((2 * half + a) * P, (2 * half + a + 1) * P)
+                nc.tensor.matmul_mx(
+                    out=bank[:, a, :],
+                    lhsT=x_codes[q][:, cols].bitcast(FP8X4),
+                    lhsT_scale=x_scales[q][:, cols],
+                    rhs=w_codes[:, 2 * P :].bitcast(FP8X4),
+                    rhs_scale=w_scales[:, 2 * P :],
+                    start=True,
+                    stop=True,
+                )
+            ysr[q, half] = bank
+
+        def do_zs(q, half):
+            if half == 0:
+                zr = work.tile([P, PACK, 2 * P], BF16, name="zr", align_bytes=64)
+                z_rows[q] = zr
+            for a in range(2):
+                t = BLOCK_T[2 * half + a]
+                nc.scalar.activation(
+                    out=z_rows[q][:, t, :], in_=ysr[q, half][:, a, :], func=ACT.Copy, scale=h32[:, q, t : t + 1]
+                )
+
+        def z_dst(q):
+            if q not in z_in:
+                zi = work.tile([P, D, PACK], BF16, name="zi", align_bytes=64)
+                z_in[q] = zi
+            return z_in[q]
+
+        def mix_z(q, eng, lo=0, hi=256):
+            dst = z_dst(q)
+            o = dst[:, 256 + lo : 256 + hi, :].rearrange("p (c i) t -> p c t i", i=4)
+            i = z_rows[q][:, :, lo:hi].rearrange("p t (c i) -> p c t i", i=4)
+            if eng == "s":
+                nc.scalar.copy(out=o, in_=i)
+            else:
+                nc.vector.tensor_copy(out=o, in_=i)
+
+        def do_tanh(q, m):
+            score = deep.tile([P, GROUP], F32, name="score")
+            nc.scalar.activation(out=score[:].rearrange("i (w e) -> i w e", e=2), in_=yts[q, m][:].rearrange("i (e w) -> i w e", e=2), func=ACT.Tanh)
+            tanhs[q, m] = score
+
+        def do_b(q, m):
+            b = deep.tile([P, GROUP], F32, name="b")
+            nc.vector.scalar_tensor_tensor(
+                out=b[:].rearrange("i (w e) -> i w e", e=2),
+                in0=tanhs[q, m][:].rearrange("i (w e) -> i w e", e=2),
+                scalar=k32[:, m : m + 1],
+                in1=yts[q, m][:].rearrange("i (e w) -> i w e", e=2),
+                op0=ALU.mult,
+                op1=ALU.add,
+            )
+            bs[q, m] = b
+
+        def do_p(q, m, eng):
+            pt = deep.tile([P, 2, P, 2], BF16, name="pt", align_bytes=64)
+            args = dict(out=pt[:], in0=bs[q, m][:].rearrange("i (u w e) -> i u w e", u=2, e=2), in1=gb[q], op=ALU.mult)
+            if eng == "g":
+                nc.gpsimd.tensor_tensor(**args)
+            else:
+                nc.vector.tensor_tensor(**args)
+            pts[q, m] = pt
+
+        def do_zt(q, m):
+            zt = deep.tile([P, 2, P, 2], BF16, name="zt", align_bytes=64)
+            nc.vector.tensor_tensor(
+                out=zt[:], in0=yts[q, m][:].rearrange("i (e u w) -> i u w e", u=2, e=2), in1=hb[q], op=ALU.mult
+            )
+            zts[q, m] = zt
+
+        def turn_i(src, q, pair):
+            bank = t_pool.tile([P, 2, 2, P], F32, name="mix")
+            for a in range(2):
+                words = src[q, 2 * pair + a][:].rearrange("i u w e -> i (u w e)").bitcast(F32)
+                for u in range(2):
+                    nc.tensor.transpose(bank[:, u, a, :], words[:, u * P : (u + 1) * P], ident[:])
+            return bank
+
+        def turn_p(q, pair):
+            turned["p", q, pair] = turn_i(pts, q, pair)
+
+        def turn_z(q, pair):
+            turned["z", q, pair] = turn_i(zts, q, pair)
+
+        def word_view(dst, pair):
+            return dst[:, pair * 2 * P : (pair + 1) * 2 * P, :].rearrange("p i t -> p (i t)").bitcast(F32).rearrange("p (r u) -> p r u", u=2)
+
+        def out_p(q, pair):
+            if q not in p_in:
+                pi = work.tile([P, D, PACK], BF16, name="pi", align_bytes=64)
+                p_in[q] = pi
+            nc.scalar.copy(out=word_view(p_in[q], pair), in_=turned["p", q, pair][:].rearrange("p u a r -> p (a r) u"))
+
+        def out_z(q, pair):
+            nc.scalar.copy(out=word_view(z_dst(q), pair), in_=turned["z", q, pair][:].rearrange("p u a r -> p (a r) u"))
+
+        def quant(store, src, q, name, lo, hi):
+            if q not in store:
+                codes = stay.tile([P, D], U32, name=name + "_codes", align_bytes=64)
+                scales = stay.tile([P, D], U8, name=name + "_scales", align_bytes=64)
+                store[q] = (codes, scales)
+            codes, scales = store[q]
+            nc.vector.quantize_mx(
+                out=codes[:, lo:hi].bitcast(FP8X4),
+                scales=scales[:, lo:hi],
+                in_=src[q][:, lo:hi, :].rearrange("p i t -> p (i t)"),
+            )
+
+        def mm_c(q, m):
+            cols = slice(m * P, (m + 1) * P)
+            nc.tensor.matmul_mx(
+                out=acc[m][:],
+                lhsT=p_q[q][0][:, cols].bitcast(FP8X4),
+                lhsT_scale=p_q[q][1][:, cols],
+                rhs=z_q[q][0][:].bitcast(FP8X4),
+                rhs_scale=z_q[q][1][:],
+                start=(q == 0),
+                stop=(q == GROUPS - 1),
+            )
+
+        acc = []
+        for m in range(M_TILES - DEFER):
+            acc_m = acc_pool.tile([P, D], F32, name="acc%d" % m)
+            acc.append(acc_m)
+
+        w_words = w_rows[:].rearrange("p m j -> p (m j)").bitcast(F32)
+        w_grouped = keep.tile([P, D, PACK], BF16, align_bytes=64)
+        w_codes = keep.tile([P, D], U32, align_bytes=64)
+        w_scales = keep.tile([P, D], U8, align_bytes=64)
+
+        def prep_w():
+            for b in range(2):
+                bank = y_pool.tile([P, 2, 2, P], F32, name="yt")
+                for a in range(2):
+                    lo = (2 * b + a) * (D // 2)
+                    for u in range(2):
+                        nc.tensor.transpose(bank[:, u, a, :], w_words[:, lo + u : lo + D // 2 : 2], ident[:])
+                i = bank[:].rearrange("p u a r -> p (a r) u")
+                if b == 0:
+                    nc.scalar.copy(out=word_view(w_grouped, b), in_=i)
+                else:
+                    nc.vector.tensor_copy(out=word_view(w_grouped, b), in_=i)
+            nc.vector.quantize_mx(
+                out=w_codes[:].bitcast(FP8X4), scales=w_scales[:], in_=w_grouped[:].rearrange("p i t -> p (i t)")
+            )
+            k_rows32 = keep.tile([P, P], F32)
+            nc.vector.tensor_copy(out=k_rows32[:], in_=k_rows[:])
+            k_bank = y_pool.tile([P, P], F32, name="yt")
+            nc.tensor.transpose(k_bank[:], k_rows32[:], ident[:])
+            nc.vector.tensor_copy(out=k32[:], in_=k_bank[:, 0:M_TILES])
+            nc.vector.tensor_copy(out=h32[:], in_=h16[:])
+
+        def mm_c_live(q, m):
+            if m < M_TILES - DEFER:
+                mm_c(q, m)
+
+        ops = {
+            "cast": lambda q, c: cast(q, c, 2),
+            "turn_x": turn_x,
+            "scale_x": scale_x,
+            "quantize_x": lambda q, c: quantize_x(q),
+            "mm_yt": mm_yt,
+            "mm_ys": mm_ys,
+            "zs": do_zs,
+            "mix_z": lambda q, c: mix_z(q, "s"),
+            "tanh": do_tanh,
+            "b": do_b,
+            "p": lambda q, m: do_p(q, m, "v" if q == GROUPS - 1 and m == 3 else "g"),
+            "zt": do_zt,
+            "turn_p": turn_p,
+            "turn_z": turn_z,
+            "out_p": out_p,
+            "out_z": out_z,
+            "quant_z": lambda q, c: quant(z_q, z_in, q, "z", 0, D),
+            "quant_p": lambda q, c: quant(p_q, p_in, q, "p", 0, D) if q < GROUPS - 1 else None,
+            "mm_c": lambda q, m: mm_c_live(q, m) if q < GROUPS - 1 else None,
+        }
+        for step in range(-3, GROUPS + 3):
+            if step == -2:
+                prep_w()
+            for name, ahead, c in TEMPLATE:
+                if 0 <= step + ahead < GROUPS:
+                    ops[name](step + ahead, c)
+
+        e = GROUPS - 1
+        for m in range(M_TILES - DEFER, M_TILES):
+            acc_m = t_pool.tile([P, D], F32, name="mix")
+            acc.append(acc_m)
+            for q in range(GROUPS - 1):
+                mm_c(q, m)
+        for m in range(M_TILES):
+            if m % 2 == 0:
+                quant(p_q, p_in, e, "p", m * P, m * P + 2 * P)
+            mm_c(e, m)
+        diag = keep.tile([P, P], F32)
+        nc.vector.tensor_scalar(out=diag[:], in0=ident[:], scalar1=ROOT_N, scalar2=None, op0=ALU.mult)
+        for m in range(M_TILES):
+            res = keep.tile([P, D], F32, name="res%d" % m)
+            lo, hi = m * P, (m + 1) * P
+            for a, b in ((0, lo), (hi, D)):
+                if a < b:
+                    nc.scalar.activation(out=res[:, a:b], in_=acc[m][:, a:b], func=ACT.Copy, scale=-1.0 / ROOT_N)
+            nc.vector.scalar_tensor_tensor(
+                out=res[:, lo:hi], in0=acc[m][:, lo:hi], scalar=-1.0 / ROOT_N, in1=diag[:], op0=ALU.mult, op1=ALU.add
+            )
+            nc.sync.dma_start(out=out[lo:hi, :], in_=res[:])

@@ -23,51 +23,69 @@ GROUPS = N // GROUP
 M_TILES = D // P
 ROOT_N = math.sqrt(N)
 BLOCK_T = (0, 2, 1, 3)
-YB, TB = 2, 3
+YB, TB, XB = 2, 2, 1
+HEAD_BANKS = {(0, 1): 0, (1, 0): 1, (1, 1): 2}
+WARM = 5
+ZT = 2
+DUP = ()
+MIXZ = "s"
+ONCE = ("turn_w", "out_w", "quant_w", "prep_k")
 DEFER = 1
 TEMPLATE = [
     ("tanh", 0, 1),
-    ("mix_z", -1, 0),
-    ("zt", 0, 1),
-    ("b", 0, 1),
-    ("mm_yt", 0, 2),
-    ("p", -1, 3),
+    ("mm_c", -2, 1),
+    ("turn_x", 2, 0),
+    ("b", 0, 0),
+    ("out_w", 1, 0),
+    ("zt", 0, 0),
     ("cast", 3, 0),
-    ("scale_x", 2, 0),
-    ("quant_z", -1, 0),
-    ("turn_p", -1, 1),
-    ("out_p", -1, 0),
-    ("p", 0, 0),
-    ("tanh", 0, 2),
-    ("turn_z", 0, 0),
-    ("b", 0, 2),
-    ("p", 0, 1),
-    ("quantize_x", 1, 0),
-    ("mm_yt", 0, 3),
-    ("mm_c", -2, 3),
-    ("turn_x", 2, 1),
-    ("out_p", -1, 1),
-    ("mm_ys", 0, 0),
-    ("out_z", 0, 0),
-    ("tanh", 0, 3),
+    ("zs", -1, 1),
     ("mm_c", -2, 2),
-    ("quant_p", -1, 0),
-    ("b", 0, 3),
-    ("cast", 3, 1),
-    ("zs", 0, 0),
-    ("scale_x", 2, 1),
-    ("mm_ys", 0, 1),
+    ("mm_c", -2, 3),
+    ("mm_c", -2, 0),
+    ("mm_yt", 0, 2),
+    ("turn_p", -1, 1),
+    ("zt", 0, 1),
+    ("p", 0, 0),
+    ("late", 0, 2),
+    ("turn_z", 0, 0),
+    ("tanh", 0, 2),
+    ("b", 0, 1),
+    ("quant_w", 1, 0),
+    ("mm_yt", 0, 3),
+    ("quantize_x", 1, 0),
+    ("scale_x", 2, 0),
+    ("p", 0, 1),
+    ("out_p", -1, 1),
+    ("b", 0, 2),
+    ("mm_ys", 0, 0),
+    ("turn_x", 2, 1),
+    ("turn_w", 2, 1),
+    ("late", 0, 0),
     ("p", 0, 2),
+    ("zt", 1, 2),
+    ("out_w", 2, 1),
+    ("mix_z", -1, 0),
+    ("quant_p", -1, 0),
+    ("turn_w", 2, 0),
+    ("prep_k", 2, 0),
     ("mm_yt", 1, 0),
-    ("mm_yt", 1, 1),
-    ("mm_c", -1, 0),
-    ("tanh", 1, 0),
-    ("b", 1, 0),
+    ("out_z", 0, 0),
+    ("quant_z", -1, 0),
+    ("late", 1, 1),
     ("turn_p", 0, 0),
-    ("mm_c", -1, 1),
-    ("zs", 0, 1),
-    ("zt", 1, 0),
-    ("turn_x", 3, 0),
+    ("tanh", 0, 3),
+    ("zs", 0, 0),
+    ("b", 0, 3),
+    ("scale_x", 2, 1),
+    ("p", 0, 3),
+    ("cast", 3, 1),
+    ("tanh", 1, 0),
+    ("out_z", -2, 1),
+    ("out_p", 0, 0),
+    ("turn_z", 0, 1),
+    ("mm_ys", 0, 1),
+    ("mm_yt", 1, 1),
 ]
 
 
@@ -80,6 +98,7 @@ def tile_extendedinfomaxnaturalgradient_t_kernel(tc, x_bytes, x_scale, w, k, g, 
         stay = ctx.enter_context(tc.tile_pool(name="stay", bufs=GROUPS if DEFER else 4))
         acc_pool = ctx.enter_context(tc.psum_pool(name="acc", bufs=1))
         y_pool = ctx.enter_context(tc.psum_pool(name="yp", bufs=YB))
+        x_pool = ctx.enter_context(tc.psum_pool(name="xp", bufs=XB))
         t_pool = ctx.enter_context(tc.psum_pool(name="tp", bufs=TB))
         ctx.enter_context(tc.manual_schedule())
 
@@ -112,7 +131,10 @@ def tile_extendedinfomaxnaturalgradient_t_kernel(tc, x_bytes, x_scale, w, k, g, 
         nc.vector.memset(k_rows[:], 0.0)
         load_x(0)
         w_rows = keep.tile([P, M_TILES, D], BF16, align_bytes=64)
-        nc.sync.dma_start(out=w_rows[:], in_=w.rearrange("(m p) j -> p m j", p=P))
+        for b in range(2):
+            nc.sync.dma_start(
+                out=w_rows[:, 2 * b : 2 * b + 2, :], in_=w[b * 2 * P : (b + 1) * 2 * P, :].rearrange("(m p) j -> p m j", p=P)
+            )
         s4 = keep.tile([P, 2, 2], F32)
         nc.sync.dma_start(out=s4[:], in_=x_scale.rearrange("o (p u e) -> p (o u) e", u=2, e=2))
         nc.sync.dma_start(out=k_rows[0:M_TILES, :], in_=k.rearrange("(m p) -> m p", p=P))
@@ -131,6 +153,13 @@ def tile_extendedinfomaxnaturalgradient_t_kernel(tc, x_bytes, x_scale, w, k, g, 
         nc.vector.memset(warm[:], 0.0)
         warm_out = keep.tile([P, 1], F32)
         nc.scalar.activation(out=warm_out[:], in_=warm[:], func=ACT.Tanh)
+        diag = keep.tile([P, P], F32)
+        nc.vector.tensor_scalar(out=diag[:], in0=ident[:], scalar1=ROOT_N, scalar2=None, op0=ALU.mult)
+        zeros = keep.tile([P, GROUP], BF16)
+        nc.vector.memset(zeros[:], 0.0)
+        idle = t_pool.tile([P, GROUP], F32, name="mix")
+        for i in range(WARM):
+            nc.tensor.matmul(out=idle[:], lhsT=zeros[:, :P], rhs=zeros[:], start=True, stop=True)
         h32 = keep.tile([P, GROUPS, PACK], F32)
         k32 = keep.tile([P, M_TILES], F32)
 
@@ -160,7 +189,10 @@ def tile_extendedinfomaxnaturalgradient_t_kernel(tc, x_bytes, x_scale, w, k, g, 
             nc.scalar.copy(out=wide[q][:, cols], in_=xb[q][:, cols].bitcast(E4M3FN))
 
         def turn_x(q, half):
-            bank = t_pool.tile([P, 2, 2, P], F32, name="mix")
+            if (q, half) in HEAD_BANKS:
+                bank = acc_pool.tile([P, 2, 2, P], F32, name="acc%d" % HEAD_BANKS[q, half])
+            else:
+                bank = x_pool.tile([P, 2, 2, P], F32, name="xt")
             words = wide[q][:].bitcast(F32)
             for a in range(2):
                 lo = BLOCK_T[2 * half + a] * (D // 2)
@@ -195,38 +227,46 @@ def tile_extendedinfomaxnaturalgradient_t_kernel(tc, x_bytes, x_scale, w, k, g, 
         def mm_yt(q, m):
             yt = y_pool.tile([P, GROUP], F32, name="yt")
             cols = slice(m * P, (m + 1) * P)
-            nc.tensor.matmul_mx(
-                out=yt[:],
-                lhsT=w_codes[:, cols].bitcast(FP8X4),
-                lhsT_scale=w_scales[:, cols],
-                rhs=x_codes[q][:].bitcast(FP8X4),
-                rhs_scale=x_scales[q][:],
-                start=True,
-                stop=True,
-            )
+            for r in range(2 if m in DUP else 1):
+                nc.tensor.matmul_mx(
+                    out=yt[:],
+                    lhsT=w_codes[:, cols].bitcast(FP8X4),
+                    lhsT_scale=w_scales[:, cols],
+                    rhs=x_codes[q][:].bitcast(FP8X4),
+                    rhs_scale=x_scales[q][:],
+                    start=True,
+                    stop=True,
+                )
             yts[q, m] = yt
 
+        ZW = D - ZT * P
+        PER = 512 // ZW if ZW else 0
+
         def mm_ys(q, half):
-            bank = t_pool.tile([P, 2, 2 * P], F32, name="mix")
-            for a in range(2):
-                cols = slice((2 * half + a) * P, (2 * half + a + 1) * P)
+            if half * PER >= PACK or not ZW:
+                return
+            bank = t_pool.tile([P, PER, ZW], F32, name="mix")
+            for a in range(PER):
+                cols = slice((PER * half + a) * P, (PER * half + a + 1) * P)
                 nc.tensor.matmul_mx(
                     out=bank[:, a, :],
                     lhsT=x_codes[q][:, cols].bitcast(FP8X4),
                     lhsT_scale=x_scales[q][:, cols],
-                    rhs=w_codes[:, 2 * P :].bitcast(FP8X4),
-                    rhs_scale=w_scales[:, 2 * P :],
+                    rhs=w_codes[:, ZT * P :].bitcast(FP8X4),
+                    rhs_scale=w_scales[:, ZT * P :],
                     start=True,
                     stop=True,
                 )
             ysr[q, half] = bank
 
         def do_zs(q, half):
+            if half * PER >= PACK or not ZW:
+                return
             if half == 0:
-                zr = work.tile([P, PACK, 2 * P], BF16, name="zr", align_bytes=64)
+                zr = work.tile([P, PACK, ZW], BF16, name="zr", align_bytes=64)
                 z_rows[q] = zr
-            for a in range(2):
-                t = BLOCK_T[2 * half + a]
+            for a in range(PER):
+                t = BLOCK_T[PER * half + a]
                 nc.scalar.activation(
                     out=z_rows[q][:, t, :], in_=ysr[q, half][:, a, :], func=ACT.Copy, scale=h32[:, q, t : t + 1]
                 )
@@ -237,14 +277,18 @@ def tile_extendedinfomaxnaturalgradient_t_kernel(tc, x_bytes, x_scale, w, k, g, 
                 z_in[q] = zi
             return z_in[q]
 
-        def mix_z(q, eng, lo=0, hi=256):
+        def mix_z(q):
+            if not ZW:
+                return
             dst = z_dst(q)
-            o = dst[:, 256 + lo : 256 + hi, :].rearrange("p (c i) t -> p c t i", i=4)
-            i = z_rows[q][:, :, lo:hi].rearrange("p t (c i) -> p c t i", i=4)
-            if eng == "s":
+            o = dst[:, ZT * P :, :].rearrange("p (c i) t -> p c t i", i=4)
+            i = z_rows[q][:].rearrange("p t (c i) -> p c t i", i=4)
+            if MIXZ == "s" and q < GROUPS - 2:
                 nc.scalar.copy(out=o, in_=i)
-            else:
+            elif MIXZ == "v" or MIXZ == "s":
                 nc.vector.tensor_copy(out=o, in_=i)
+            else:
+                nc.gpsimd.tensor_scalar(out=o, in0=i, scalar1=1.0, scalar2=0.0, op0=ALU.mult, op1=ALU.add)
 
         def do_tanh(q, m):
             score = deep.tile([P, GROUP], F32, name="score")
@@ -279,19 +323,20 @@ def tile_extendedinfomaxnaturalgradient_t_kernel(tc, x_bytes, x_scale, w, k, g, 
             )
             zts[q, m] = zt
 
-        def turn_i(src, q, pair):
+        def turn_i(src, q, pair, count):
             bank = t_pool.tile([P, 2, 2, P], F32, name="mix")
-            for a in range(2):
+            for a in range(count):
                 words = src[q, 2 * pair + a][:].rearrange("i u w e -> i (u w e)").bitcast(F32)
                 for u in range(2):
                     nc.tensor.transpose(bank[:, u, a, :], words[:, u * P : (u + 1) * P], ident[:])
             return bank
 
         def turn_p(q, pair):
-            turned["p", q, pair] = turn_i(pts, q, pair)
+            turned["p", q, pair] = turn_i(pts, q, pair, 2)
 
         def turn_z(q, pair):
-            turned["z", q, pair] = turn_i(zts, q, pair)
+            if 2 * pair < ZT:
+                turned["z", q, pair] = turn_i(zts, q, pair, min(2, ZT - 2 * pair))
 
         def word_view(dst, pair):
             return dst[:, pair * 2 * P : (pair + 1) * 2 * P, :].rearrange("p i t -> p (i t)").bitcast(F32).rearrange("p (r u) -> p r u", u=2)
@@ -303,7 +348,13 @@ def tile_extendedinfomaxnaturalgradient_t_kernel(tc, x_bytes, x_scale, w, k, g, 
             nc.scalar.copy(out=word_view(p_in[q], pair), in_=turned["p", q, pair][:].rearrange("p u a r -> p (a r) u"))
 
         def out_z(q, pair):
-            nc.scalar.copy(out=word_view(z_dst(q), pair), in_=turned["z", q, pair][:].rearrange("p u a r -> p (a r) u"))
+            if 2 * pair < ZT:
+                count = min(2, ZT - 2 * pair)
+                dst = z_dst(q)[:, 2 * pair * P : (2 * pair + count) * P, :].rearrange("p i t -> p (i t)").bitcast(F32)
+                nc.scalar.copy(
+                    out=dst.rearrange("p (r u) -> p r u", u=2),
+                    in_=turned["z", q, pair][:].rearrange("p u a r -> p u (a r)")[:, :, : count * P].rearrange("p u r -> p r u"),
+                )
 
         def quant(store, src, q, name, lo, hi):
             if q not in store:
@@ -318,6 +369,12 @@ def tile_extendedinfomaxnaturalgradient_t_kernel(tc, x_bytes, x_scale, w, k, g, 
             )
 
         def mm_c(q, m):
+            if m not in acc:
+                if m < M_TILES - DEFER:
+                    acc_m = acc_pool.tile([P, D], F32, name="acc%d" % m)
+                else:
+                    acc_m = x_pool.tile([P, D], F32, name="xt")
+                acc[m] = acc_m
             cols = slice(m * P, (m + 1) * P)
             nc.tensor.matmul_mx(
                 out=acc[m][:],
@@ -329,34 +386,39 @@ def tile_extendedinfomaxnaturalgradient_t_kernel(tc, x_bytes, x_scale, w, k, g, 
                 stop=(q == GROUPS - 1),
             )
 
-        acc = []
-        for m in range(M_TILES - DEFER):
-            acc_m = acc_pool.tile([P, D], F32, name="acc%d" % m)
-            acc.append(acc_m)
+        acc = {}
 
         w_words = w_rows[:].rearrange("p m j -> p (m j)").bitcast(F32)
         w_grouped = keep.tile([P, D, PACK], BF16, align_bytes=64)
         w_codes = keep.tile([P, D], U32, align_bytes=64)
         w_scales = keep.tile([P, D], U8, align_bytes=64)
 
-        def prep_w():
-            for b in range(2):
-                bank = y_pool.tile([P, 2, 2, P], F32, name="yt")
-                for a in range(2):
-                    lo = (2 * b + a) * (D // 2)
-                    for u in range(2):
-                        nc.tensor.transpose(bank[:, u, a, :], w_words[:, lo + u : lo + D // 2 : 2], ident[:])
-                i = bank[:].rearrange("p u a r -> p (a r) u")
-                if b == 0:
-                    nc.scalar.copy(out=word_view(w_grouped, b), in_=i)
-                else:
-                    nc.vector.tensor_copy(out=word_view(w_grouped, b), in_=i)
+        w_banks = {}
+
+        def turn_w(q, b):
+            bank = y_pool.tile([P, 2, 2, P], F32, name="yt")
+            for a in range(2):
+                lo = (2 * b + a) * (D // 2)
+                for u in range(2):
+                    nc.tensor.transpose(bank[:, u, a, :], w_words[:, lo + u : lo + D // 2 : 2], ident[:])
+            w_banks[b] = bank
+
+        def out_w(q, b):
+            i = w_banks[b][:].rearrange("p u a r -> p (a r) u")
+            if b == 0:
+                nc.scalar.copy(out=word_view(w_grouped, b), in_=i)
+            else:
+                nc.vector.tensor_copy(out=word_view(w_grouped, b), in_=i)
+
+        def quant_w(q, b):
             nc.vector.quantize_mx(
                 out=w_codes[:].bitcast(FP8X4), scales=w_scales[:], in_=w_grouped[:].rearrange("p i t -> p (i t)")
             )
-            k_rows32 = keep.tile([P, P], F32)
+
+        def prep_k(q, b):
+            k_rows32 = keep.tile([P, P], F32, name="k_rows32")
             nc.vector.tensor_copy(out=k_rows32[:], in_=k_rows[:])
-            k_bank = y_pool.tile([P, P], F32, name="yt")
+            k_bank = x_pool.tile([P, P], F32, name="xt")
             nc.tensor.transpose(k_bank[:], k_rows32[:], ident[:])
             nc.vector.tensor_copy(out=k32[:], in_=k_bank[:, 0:M_TILES])
             nc.vector.tensor_copy(out=h32[:], in_=h16[:])
@@ -366,6 +428,10 @@ def tile_extendedinfomaxnaturalgradient_t_kernel(tc, x_bytes, x_scale, w, k, g, 
                 mm_c(q, m)
 
         ops = {
+            "turn_w": turn_w,
+            "out_w": out_w,
+            "quant_w": quant_w,
+            "prep_k": prep_k,
             "cast": lambda q, c: cast(q, c, 2),
             "turn_x": turn_x,
             "scale_x": scale_x,
@@ -373,11 +439,11 @@ def tile_extendedinfomaxnaturalgradient_t_kernel(tc, x_bytes, x_scale, w, k, g, 
             "mm_yt": mm_yt,
             "mm_ys": mm_ys,
             "zs": do_zs,
-            "mix_z": lambda q, c: mix_z(q, "s"),
+            "mix_z": lambda q, c: mix_z(q),
             "tanh": do_tanh,
             "b": do_b,
             "p": lambda q, m: do_p(q, m, "v" if q == GROUPS - 1 and m == 3 else "g"),
-            "zt": do_zt,
+            "zt": lambda q, m: do_zt(q, m) if m < ZT else None,
             "turn_p": turn_p,
             "turn_z": turn_z,
             "out_p": out_p,
@@ -386,31 +452,39 @@ def tile_extendedinfomaxnaturalgradient_t_kernel(tc, x_bytes, x_scale, w, k, g, 
             "quant_p": lambda q, c: quant(p_q, p_in, q, "p", 0, D) if q < GROUPS - 1 else None,
             "mm_c": lambda q, m: mm_c_live(q, m) if q < GROUPS - 1 else None,
         }
+        late = []
+
+        def catch_up(q, c):
+            if GROUPS - 1 not in x_codes:
+                return
+            for i in range(2):
+                if len(late) < GROUPS - 1 and len(late) in p_q and len(late) in z_q:
+                    mm_c(len(late), M_TILES - 1)
+                    late.append(0)
+
+        ops["late"] = catch_up
         for step in range(-3, GROUPS + 3):
-            if step == -2:
-                prep_w()
             for name, ahead, c in TEMPLATE:
-                if 0 <= step + ahead < GROUPS:
-                    ops[name](step + ahead, c)
+                q = step + ahead
+                if 0 <= q < GROUPS and (q == 0 or name not in ONCE):
+                    ops[name](q, c)
 
         e = GROUPS - 1
-        for m in range(M_TILES - DEFER, M_TILES):
-            acc_m = t_pool.tile([P, D], F32, name="mix")
-            acc.append(acc_m)
-            for q in range(GROUPS - 1):
-                mm_c(q, m)
+        for q in range(len(late), GROUPS - 1):
+            mm_c(q, M_TILES - 1)
         for m in range(M_TILES):
             if m % 2 == 0:
                 quant(p_q, p_in, e, "p", m * P, m * P + 2 * P)
             mm_c(e, m)
-        diag = keep.tile([P, P], F32)
-        nc.vector.tensor_scalar(out=diag[:], in0=ident[:], scalar1=ROOT_N, scalar2=None, op0=ALU.mult)
         for m in range(M_TILES):
             res = keep.tile([P, D], F32, name="res%d" % m)
             lo, hi = m * P, (m + 1) * P
             for a, b in ((0, lo), (hi, D)):
                 if a < b:
-                    nc.scalar.activation(out=res[:, a:b], in_=acc[m][:, a:b], func=ACT.Copy, scale=-1.0 / ROOT_N)
+                    if m % 2 == 0:
+                        nc.vector.tensor_scalar(out=res[:, a:b], in0=acc[m][:, a:b], scalar1=-1.0 / ROOT_N, scalar2=None, op0=ALU.mult)
+                    else:
+                        nc.scalar.activation(out=res[:, a:b], in_=acc[m][:, a:b], func=ACT.Copy, scale=-1.0 / ROOT_N)
             nc.vector.scalar_tensor_tensor(
                 out=res[:, lo:hi], in0=acc[m][:, lo:hi], scalar=-1.0 / ROOT_N, in1=diag[:], op0=ALU.mult, op1=ALU.add
             )

import math
from contextlib import ExitStack

import concourse.mybir as mybir
from concourse.masks import make_identity

N, D = 8192, 512
FLOPS = 2 * (2 * N * D * D)

F32 = mybir.dt.float32
BF16 = mybir.dt.bfloat16
U32 = mybir.dt.uint32
U8 = mybir.dt.uint8
E4M3FN = mybir.dt.float8_e4m3fn
FP8X4 = mybir.dt.float8_e4m3fn_x4
ACT = mybir.ActivationFunctionType
ALU = mybir.AluOpType

P = 128
PACK = 4
GROUP = P * PACK
GROUPS = N // GROUP
M_TILES = D // P
ROOT_N = math.sqrt(N)
BLOCK_T = (0, 2, 1, 3)
YB, TB, XB = 2, 2, 1
HEAD_BANKS = {(0, 1): 0, (1, 0): 1, (1, 1): 2}
WARM = 5
ZT = 2
DUP = ()
MIXZ = "s"
ONCE = ("turn_w", "out_w", "quant_w", "prep_k")
DEFER = 1
TEMPLATE = [
    ("tanh", 0, 1),
    ("mm_c", -2, 1),
    ("turn_x", 2, 0),
    ("b", 0, 0),
    ("out_w", 1, 0),
    ("zt", 0, 0),
    ("cast", 3, 0),
    ("zs", -1, 1),
    ("mm_c", -2, 2),
    ("mm_c", -2, 3),
    ("mm_c", -2, 0),
    ("mm_yt", 0, 2),
    ("turn_p", -1, 1),
    ("zt", 0, 1),
    ("p", 0, 0),
    ("late", 0, 2),
    ("turn_z", 0, 0),
    ("tanh", 0, 2),
    ("b", 0, 1),
    ("quant_w", 1, 0),
    ("mm_yt", 0, 3),
    ("quantize_x", 1, 0),
    ("scale_x", 2, 0),
    ("p", 0, 1),
    ("out_p", -1, 1),
    ("b", 0, 2),
    ("mm_ys", 0, 0),
    ("turn_x", 2, 1),
    ("turn_w", 2, 1),
    ("late", 0, 0),
    ("p", 0, 2),
    ("zt", 1, 2),
    ("out_w", 2, 1),
    ("mix_z", -1, 0),
    ("quant_p", -1, 0),
    ("turn_w", 2, 0),
    ("prep_k", 2, 0),
    ("mm_yt", 1, 0),
    ("out_z", 0, 0),
    ("quant_z", -1, 0),
    ("late", 1, 1),
    ("turn_p", 0, 0),
    ("tanh", 0, 3),
    ("zs", 0, 0),
    ("b", 0, 3),
    ("scale_x", 2, 1),
    ("p", 0, 3),
    ("cast", 3, 1),
    ("tanh", 1, 0),
    ("out_z", -2, 1),
    ("out_p", 0, 0),
    ("turn_z", 0, 1),
    ("mm_ys", 0, 1),
    ("mm_yt", 1, 1),
]


def tile_extendedinfomaxnaturalgradient_t_kernel(tc, x_bytes, x_scale, w, k, g, h, out):
    nc = tc.nc
    with ExitStack() as ctx:
        keep = ctx.enter_context(tc.tile_pool(name="keep", bufs=1))
        work = ctx.enter_context(tc.tile_pool(name="work", bufs=2))
        deep = ctx.enter_context(tc.tile_pool(name="deep", bufs=3))
        stay = ctx.enter_context(tc.tile_pool(name="stay", bufs=GROUPS if DEFER else 4))
        acc_pool = ctx.enter_context(tc.psum_pool(name="acc", bufs=1))
        y_pool = ctx.enter_context(tc.psum_pool(name="yp", bufs=YB))
        x_pool = ctx.enter_context(tc.psum_pool(name="xp", bufs=XB))
        t_pool = ctx.enter_context(tc.psum_pool(name="tp", bufs=TB))
        ctx.enter_context(tc.manual_schedule())

        x_view = x_bytes.rearrange("(g p t) k -> p g (t k)", p=P, t=PACK)
        chunks = [(0, 1), (1, 2), (2, 4), (4, 8), (8, 12), (12, 16)]
        xb = {}

        def load_x(c):
            lo, hi = chunks[c]
            xbytes = keep.tile([P, hi - lo, PACK * D], U8, name="xbytes%d" % c, align_bytes=64)
            nc.sync.dma_start(out=xbytes[:], in_=x_view[:, lo:hi, :])
            for q in range(lo, hi):
                xb[q] = xbytes[:, q - lo, :]

        gb = {}
        hb = {}

        def load_gains(c):
            lo, hi = chunks[c]
            g_b = keep.tile([P, hi - lo, GROUP], BF16, name="gb%d" % c)
            h_b = keep.tile([P, hi - lo, GROUP], BF16, name="hb%d" % c)
            rows = slice(lo * GROUP, hi * GROUP)
            nc.sync.dma_start(out=g_b[:].rearrange("p a n -> p (a n)"), in_=g[rows].partition_broadcast(P))
            nc.sync.dma_start(out=h_b[:].rearrange("p a n -> p (a n)"), in_=h[rows].partition_broadcast(P))
            for q in range(lo, hi):
                gb[q] = g_b[:, q - lo, :].rearrange("i (w u e) -> i u w e", u=2, e=2)
                hb[q] = h_b[:, q - lo, :].rearrange("i (w u e) -> i u w e", u=2, e=2)

        k_rows = keep.tile([P, P], BF16)
        nc.vector.memset(k_rows[:], 0.0)
        load_x(0)
        w_rows = keep.tile([P, M_TILES, D], BF16, align_bytes=64)
        for b in range(2):
            nc.sync.dma_start(
                out=w_rows[:, 2 * b : 2 * b + 2, :], in_=w[b * 2 * P : (b + 1) * 2 * P, :].rearrange("(m p) j -> p m j", p=P)
            )
        s4 = keep.tile([P, 2, 2], F32)
        nc.sync.dma_start(out=s4[:], in_=x_scale.rearrange("o (p u e) -> p (o u) e", u=2, e=2))
        nc.sync.dma_start(out=k_rows[0:M_TILES, :], in_=k.rearrange("(m p) -> m p", p=P))
        load_x(1)
        load_gains(0)
        load_gains(1)
        h16 = keep.tile([P, GROUPS, PACK], BF16)
        nc.scalar.dma_start(out=h16[:], in_=h.rearrange("(g p t) -> p g t", p=P, t=PACK))
        for c in range(2, len(chunks)):
            load_x(c)
            load_gains(c)

        ident = keep.tile([P, P], F32)
        make_identity(nc, ident[:])
        warm = keep.tile([P, 1], F32)
        nc.vector.memset(warm[:], 0.0)
        warm_out = keep.tile([P, 1], F32)
        nc.scalar.activation(out=warm_out[:], in_=warm[:], func=ACT.Tanh)
        diag = keep.tile([P, P], F32)
        nc.vector.tensor_scalar(out=diag[:], in0=ident[:], scalar1=ROOT_N, scalar2=None, op0=ALU.mult)
        zeros = keep.tile([P, GROUP], BF16)
        nc.vector.memset(zeros[:], 0.0)
        idle = t_pool.tile([P, GROUP], F32, name="mix")
        for i in range(WARM):
            nc.tensor.matmul(out=idle[:], lhsT=zeros[:, :P], rhs=zeros[:], start=True, stop=True)
        h32 = keep.tile([P, GROUPS, PACK], F32)
        k32 = keep.tile([P, M_TILES], F32)

        wide = {}
        grouped = {}
        x_codes = {}
        x_scales = {}
        turned = {}
        yts = {}
        ysr = {}
        tanhs = {}
        bs = {}
        pts = {}
        zts = {}
        p_in = {}
        z_in = {}
        z_rows = {}
        p_q = {}
        z_q = {}

        def cast(q, c, pieces):
            if c == 0:
                x_wide = deep.tile([P, PACK * D], BF16, name="x_wide", align_bytes=64)
                wide[q] = x_wide
            step = PACK * D // pieces
            cols = slice(c * step, (c + 1) * step)
            nc.scalar.copy(out=wide[q][:, cols], in_=xb[q][:, cols].bitcast(E4M3FN))

        def turn_x(q, half):
            if (q, half) in HEAD_BANKS:
                bank = acc_pool.tile([P, 2, 2, P], F32, name="acc%d" % HEAD_BANKS[q, half])
            else:
                bank = x_pool.tile([P, 2, 2, P], F32, name="xt")
            words = wide[q][:].bitcast(F32)
            for a in range(2):
                lo = BLOCK_T[2 * half + a] * (D // 2)
                for u in range(2):
                    nc.tensor.transpose(bank[:, u, a, :], words[:, lo + u : lo + D // 2 : 2], ident[:])
            turned[q, half] = bank

        def scale_x(q, half):
            if half == 0:
                x_grouped = work.tile([P, GROUP, 2, 2], BF16, name="x_grouped", align_bytes=64)
                grouped[q] = x_grouped
            rows = slice(half * 2 * P, (half + 1) * 2 * P)
            bank = turned[q, half][:].rearrange("p u a r -> p (u a r)").bitcast(BF16)
            nc.vector.tensor_tensor(
                out=grouped[q][:, rows, :, :],
                in0=bank.rearrange("p (u r e) -> p r u e", u=2, e=2),
                in1=s4[:].unsqueeze(1).to_broadcast([P, 2 * P, 2, 2]),
                op=ALU.mult,
            )

        def quantize_x(q):
            codes = deep.tile([P, GROUP], U32, name="x_codes", align_bytes=64)
            scales = deep.tile([P, GROUP], U8, name="x_scales", align_bytes=64)
            nc.vector.quantize_mx(
                out=codes[:].bitcast(FP8X4),
                scales=scales[:],
                in_=grouped[q][:].rearrange("p r u e -> p (r u e)"),
            )
            x_codes[q] = codes
            x_scales[q] = scales

        def mm_yt(q, m):
            yt = y_pool.tile([P, GROUP], F32, name="yt")
            cols = slice(m * P, (m + 1) * P)
            for r in range(2 if m in DUP else 1):
                nc.tensor.matmul_mx(
                    out=yt[:],
                    lhsT=w_codes[:, cols].bitcast(FP8X4),
                    lhsT_scale=w_scales[:, cols],
                    rhs=x_codes[q][:].bitcast(FP8X4),
                    rhs_scale=x_scales[q][:],
                    start=True,
                    stop=True,
                )
            yts[q, m] = yt

        ZW = D - ZT * P
        PER = 512 // ZW if ZW else 0

        def mm_ys(q, half):
            if half * PER >= PACK or not ZW:
                return
            bank = t_pool.tile([P, PER, ZW], F32, name="mix")
            for a in range(PER):
                cols = slice((PER * half + a) * P, (PER * half + a + 1) * P)
                nc.tensor.matmul_mx(
                    out=bank[:, a, :],
                    lhsT=x_codes[q][:, cols].bitcast(FP8X4),
                    lhsT_scale=x_scales[q][:, cols],
                    rhs=w_codes[:, ZT * P :].bitcast(FP8X4),
                    rhs_scale=w_scales[:, ZT * P :],
                    start=True,
                    stop=True,
                )
            ysr[q, half] = bank

        def do_zs(q, half):
            if half * PER >= PACK or not ZW:
                return
            if half == 0:
                zr = work.tile([P, PACK, ZW], BF16, name="zr", align_bytes=64)
                z_rows[q] = zr
            for a in range(PER):
                t = BLOCK_T[PER * half + a]
                nc.scalar.activation(
                    out=z_rows[q][:, t, :], in_=ysr[q, half][:, a, :], func=ACT.Copy, scale=h32[:, q, t : t + 1]
                )

        def z_dst(q):
            if q not in z_in:
                zi = work.tile([P, D, PACK], BF16, name="zi", align_bytes=64)
                z_in[q] = zi
            return z_in[q]

        def mix_z(q):
            if not ZW:
                return
            dst = z_dst(q)
            o = dst[:, ZT * P :, :].rearrange("p (c i) t -> p c t i", i=4)
            i = z_rows[q][:].rearrange("p t (c i) -> p c t i", i=4)
            if MIXZ == "s" and q < GROUPS - 2:
                nc.scalar.copy(out=o, in_=i)
            elif MIXZ == "v" or MIXZ == "s":
                nc.vector.tensor_copy(out=o, in_=i)
            else:
                nc.gpsimd.tensor_scalar(out=o, in0=i, scalar1=1.0, scalar2=0.0, op0=ALU.mult, op1=ALU.add)

        def do_tanh(q, m):
            score = deep.tile([P, GROUP], F32, name="score")
            nc.scalar.activation(out=score[:].rearrange("i (w e) -> i w e", e=2), in_=yts[q, m][:].rearrange("i (e w) -> i w e", e=2), func=ACT.Tanh)
            tanhs[q, m] = score

        def do_b(q, m):
            b = deep.tile([P, GROUP], F32, name="b")
            nc.vector.scalar_tensor_tensor(
                out=b[:].rearrange("i (w e) -> i w e", e=2),
                in0=tanhs[q, m][:].rearrange("i (w e) -> i w e", e=2),
                scalar=k32[:, m : m + 1],
                in1=yts[q, m][:].rearrange("i (e w) -> i w e", e=2),
                op0=ALU.mult,
                op1=ALU.add,
            )
            bs[q, m] = b

        def do_p(q, m, eng):
            pt = deep.tile([P, 2, P, 2], BF16, name="pt", align_bytes=64)
            args = dict(out=pt[:], in0=bs[q, m][:].rearrange("i (u w e) -> i u w e", u=2, e=2), in1=gb[q], op=ALU.mult)
            if eng == "g":
                nc.gpsimd.tensor_tensor(**args)
            else:
                nc.vector.tensor_tensor(**args)
            pts[q, m] = pt

        def do_zt(q, m):
            zt = deep.tile([P, 2, P, 2], BF16, name="zt", align_bytes=64)
            nc.vector.tensor_tensor(
                out=zt[:], in0=yts[q, m][:].rearrange("i (e u w) -> i u w e", u=2, e=2), in1=hb[q], op=ALU.mult
            )
            zts[q, m] = zt

        def turn_i(src, q, pair, count):
            bank = t_pool.tile([P, 2, 2, P], F32, name="mix")
            for a in range(count):
                words = src[q, 2 * pair + a][:].rearrange("i u w e -> i (u w e)").bitcast(F32)
                for u in range(2):
                    nc.tensor.transpose(bank[:, u, a, :], words[:, u * P : (u + 1) * P], ident[:])
            return bank

        def turn_p(q, pair):
            turned["p", q, pair] = turn_i(pts, q, pair, 2)

        def turn_z(q, pair):
            if 2 * pair < ZT:
                turned["z", q, pair] = turn_i(zts, q, pair, min(2, ZT - 2 * pair))

        def word_view(dst, pair):
            return dst[:, pair * 2 * P : (pair + 1) * 2 * P, :].rearrange("p i t -> p (i t)").bitcast(F32).rearrange("p (r u) -> p r u", u=2)

        def out_p(q, pair):
            if q not in p_in:
                pi = work.tile([P, D, PACK], BF16, name="pi", align_bytes=64)
                p_in[q] = pi
            nc.scalar.copy(out=word_view(p_in[q], pair), in_=turned["p", q, pair][:].rearrange("p u a r -> p (a r) u"))

        def out_z(q, pair):
            if 2 * pair < ZT:
                count = min(2, ZT - 2 * pair)
                dst = z_dst(q)[:, 2 * pair * P : (2 * pair + count) * P, :].rearrange("p i t -> p (i t)").bitcast(F32)
                nc.scalar.copy(
                    out=dst.rearrange("p (r u) -> p r u", u=2),
                    in_=turned["z", q, pair][:].rearrange("p u a r -> p u (a r)")[:, :, : count * P].rearrange("p u r -> p r u"),
                )

        def quant(store, src, q, name, lo, hi):
            if q not in store:
                codes = stay.tile([P, D], U32, name=name + "_codes", align_bytes=64)
                scales = stay.tile([P, D], U8, name=name + "_scales", align_bytes=64)
                store[q] = (codes, scales)
            codes, scales = store[q]
            nc.vector.quantize_mx(
                out=codes[:, lo:hi].bitcast(FP8X4),
                scales=scales[:, lo:hi],
                in_=src[q][:, lo:hi, :].rearrange("p i t -> p (i t)"),
            )

        def mm_c(q, m):
            if m not in acc:
                if m < M_TILES - DEFER:
                    acc_m = acc_pool.tile([P, D], F32, name="acc%d" % m)
                else:
                    acc_m = x_pool.tile([P, D], F32, name="xt")
                acc[m] = acc_m
            cols = slice(m * P, (m + 1) * P)
            nc.tensor.matmul_mx(
                out=acc[m][:],
                lhsT=p_q[q][0][:, cols].bitcast(FP8X4),
                lhsT_scale=p_q[q][1][:, cols],
                rhs=z_q[q][0][:].bitcast(FP8X4),
                rhs_scale=z_q[q][1][:],
                start=(q == 0),
                stop=(q == GROUPS - 1),
            )

        acc = {}

        w_words = w_rows[:].rearrange("p m j -> p (m j)").bitcast(F32)
        w_grouped = keep.tile([P, D, PACK], BF16, align_bytes=64)
        w_codes = keep.tile([P, D], U32, align_bytes=64)
        w_scales = keep.tile([P, D], U8, align_bytes=64)

        w_banks = {}

        def turn_w(q, b):
            bank = y_pool.tile([P, 2, 2, P], F32, name="yt")
            for a in range(2):
                lo = (2 * b + a) * (D // 2)
                for u in range(2):
                    nc.tensor.transpose(bank[:, u, a, :], w_words[:, lo + u : lo + D // 2 : 2], ident[:])
            w_banks[b] = bank

        def out_w(q, b):
            i = w_banks[b][:].rearrange("p u a r -> p (a r) u")
            if b == 0:
                nc.scalar.copy(out=word_view(w_grouped, b), in_=i)
            else:
                nc.vector.tensor_copy(out=word_view(w_grouped, b), in_=i)

        def quant_w(q, b):
            nc.vector.quantize_mx(
                out=w_codes[:].bitcast(FP8X4), scales=w_scales[:], in_=w_grouped[:].rearrange("p i t -> p (i t)")
            )

        def prep_k(q, b):
            k_rows32 = keep.tile([P, P], F32, name="k_rows32")
            nc.vector.tensor_copy(out=k_rows32[:], in_=k_rows[:])
            k_bank = x_pool.tile([P, P], F32, name="xt")
            nc.tensor.transpose(k_bank[:], k_rows32[:], ident[:])
            nc.vector.tensor_copy(out=k32[:], in_=k_bank[:, 0:M_TILES])
            nc.vector.tensor_copy(out=h32[:], in_=h16[:])

        def mm_c_live(q, m):
            if m < M_TILES - DEFER:
                mm_c(q, m)

        ops = {
            "turn_w": turn_w,
            "out_w": out_w,
            "quant_w": quant_w,
            "prep_k": prep_k,
            "cast": lambda q, c: cast(q, c, 2),
            "turn_x": turn_x,
            "scale_x": scale_x,
            "quantize_x": lambda q, c: quantize_x(q),
            "mm_yt": mm_yt,
            "mm_ys": mm_ys,
            "zs": do_zs,
            "mix_z": lambda q, c: mix_z(q),
            "tanh": do_tanh,
            "b": do_b,
            "p": lambda q, m: do_p(q, m, "v" if q == GROUPS - 1 and m == 3 else "g"),
            "zt": lambda q, m: do_zt(q, m) if m < ZT else None,
            "turn_p": turn_p,
            "turn_z": turn_z,
            "out_p": out_p,
            "out_z": out_z,
            "quant_z": lambda q, c: quant(z_q, z_in, q, "z", 0, D),
            "quant_p": lambda q, c: quant(p_q, p_in, q, "p", 0, D) if q < GROUPS - 1 else None,
            "mm_c": lambda q, m: mm_c_live(q, m) if q < GROUPS - 1 else None,
        }
        late = []

        def catch_up(q, c):
            if GROUPS - 1 not in x_codes:
                return
            for i in range(2):
                if len(late) < GROUPS - 1 and len(late) in p_q and len(late) in z_q:
                    mm_c(len(late), M_TILES - 1)
                    late.append(0)

        ops["late"] = catch_up
        for step in range(-3, GROUPS + 3):
            for name, ahead, c in TEMPLATE:
                q = step + ahead
                if 0 <= q < GROUPS and (q == 0 or name not in ONCE):
                    ops[name](q, c)

        e = GROUPS - 1
        for q in range(len(late), GROUPS - 1):
            mm_c(q, M_TILES - 1)
        for m in range(M_TILES):
            if m % 2 == 0:
                quant(p_q, p_in, e, "p", m * P, m * P + 2 * P)
            mm_c(e, m)
        for m in range(M_TILES):
            res = keep.tile([P, D], F32, name="res%d" % m)
            lo, hi = m * P, (m + 1) * P
            for a, b in ((0, lo), (hi, D)):
                if a < b:
                    if m % 2 == 0:
                        nc.vector.tensor_scalar(out=res[:, a:b], in0=acc[m][:, a:b], scalar1=-1.0 / ROOT_N, scalar2=None, op0=ALU.mult)
                    else:
                        nc.scalar.activation(out=res[:, a:b], in_=acc[m][:, a:b], func=ACT.Copy, scale=-1.0 / ROOT_N)
            nc.vector.scalar_tensor_tensor(
                out=res[:, lo:hi], in0=acc[m][:, lo:hi], scalar=-1.0 / ROOT_N, in1=diag[:], op0=ALU.mult, op1=ALU.add
            )
            nc.sync.dma_start(out=out[lo:hi, :], in_=res[:])
